import numpy as np
import ml_dtypes


def mxq(x, axis, fmt="e4m3"):
    dtype, down = {"e4m3": (ml_dtypes.float8_e4m3fn, 7), "e5m2": (ml_dtypes.float8_e5m2, 14)}[fmt]
    v = np.moveaxis(np.asarray(x, np.float32).astype(ml_dtypes.bfloat16).astype(np.float64), axis, -1)
    blocks = v.reshape(v.shape[:-1] + (-1, 32))
    amax = np.abs(blocks).max(-1, keepdims=True)
    byte = np.maximum(np.where(amax > 0, np.frexp(amax)[1] - 1 + 127, 0) - down, 1)
    scale = np.exp2(byte - 127.0)
    codes = (blocks / scale).astype(np.float32).astype(dtype).astype(np.float64)
    return np.moveaxis((codes * scale).reshape(v.shape), -1, axis)


WIDE = False


def mx_kscale(k):
    if not WIDE:
        return np.ones(k)
    levels = np.array([30, -30])
    if k % 512:
        return np.exp2(np.random.permutation(np.resize(levels, k // 32))).repeat(32)
    a = np.empty((k // 512, 16))
    for p in range(k // 512):
        a[p, :8] = np.random.permutation(np.resize(levels, 8))
        for g in range(8):
            far = levels[np.abs(levels - a[p, g]) >= 10]
            a[p, g + 8] = far[np.random.randint(len(far))]
    return np.exp2(a.ravel()).repeat(32)


def f64(x):
    return np.asarray(x).astype(np.float64)


def striped(idx):
    return np.tile(np.asarray(idx).reshape(-1, 16).T, (8, 1)).astype(np.uint16)


def unstriped(offs):
    return offs[:16].T.reshape(-1).astype(np.int64)


K, N, T, J = 512, 512, 2048, 512


def setup_inputs():
    n = np.random.standard_normal
    idx = np.random.permutation(T)[:J]
    fj = mx_kscale(J)
    tj = np.ones(T)
    tj[idx] = fj
    return {
        "xt": (n((K, T)) * tj).astype(np.float32),
        "g": (n((N, T)) * np.exp(0.5 * n((1, T))) / tj).astype(np.float32),
        "old": (1.0 * n((K, N))).astype(np.float32),
        "offs": striped(idx),
    }


def reference(xt, g, old, offs):
    idx = unstriped(offs)
    xj = f64(xt)[:, idx].T
    gj = f64(g)[:, idx].T
    xjq = mxq(xj, 0, "e4m3")
    gjq = mxq(gj, 0, "e5m2")
    w0 = xjq.T @ gjq
    w = 0.04 * w0
    y = w * 1.0 / np.sqrt(np.mean(np.square(w), axis=1, keepdims=True) + 0.01) - 0.1 * f64(old)
    return y

from contextlib import ExitStack

import concourse.mybir as mybir
from concourse.masks import make_identity

K, N, T, J = 512, 512, 2048, 512
FLOPS = 2 * K * N * J

F32 = mybir.dt.float32
BF16 = mybir.dt.bfloat16
U32 = mybir.dt.uint32
U16 = mybir.dt.uint16
U8 = mybir.dt.uint8
E4M3 = mybir.dt.float8_e4m3fn_x4
E5M2 = mybir.dt.float8_e5m2_x4
ALU = mybir.AluOpType
ACT = mybir.ActivationFunctionType

P = 128
TILES = 4


def tile_list_wgrad_rownormed_kernel(tc, xt, g, old, offs, out):
    nc = tc.nc
    with ExitStack() as ctx:
        keep = ctx.enter_context(tc.tile_pool(name="keep", bufs=1))
        ring = ctx.enter_context(tc.tile_pool(name="ring", bufs=3))
        turn = ctx.enter_context(tc.psum_pool(name="turn", bufs=3))
        sums = ctx.enter_context(tc.psum_pool(name="sums", bufs=1))

        def rows(i):
            return slice(i * P, (i + 1) * P)

        offsets = keep.tile([P, J // 16], U16, name="offsets")
        g_raw = [keep.tile([P, T], F32, name="g_raw%d" % i) for i in range(TILES)]
        x_raw = [
            keep.tile([P, T], F32, name="x_raw%d" % i, tag="x%d" % i, align_bytes=64)
            for i in range(TILES)
        ]
        old_raw = [keep.tile([P, N], F32, name="old_raw%d" % i) for i in range(TILES)]

        nc.sync.dma_start(g_raw[0][:], g[rows(0), :])
        nc.sync.dma_start(offsets[:], offs)
        for i in range(1, TILES):
            nc.sync.dma_start(g_raw[i][:], g[rows(i), :])
        for i in range(TILES):
            nc.sync.dma_start(x_raw[i][:], xt[rows(i), :])
        for i in (2, 0, 1, 3):
            nc.sync.dma_start(old_raw[i][:], old[rows(i), :])

        ident = keep.tile([P, P], F32, name="ident")
        make_identity(nc, ident[:])
        floor = keep.tile([P, 1], F32, name="floor")
        nc.gpsimd.memset(floor[:], 6.25)
        warm = keep.tile([P, 1], F32, name="warm")
        nc.scalar.activation(warm[:], floor[:], ACT.Abs_reciprocal_sqrt, bias=floor[:])

        def gather_and_turn(raw, grouped):
            picked = ring.tile([P, J], BF16, name="picked", align_bytes=64)
            nc.vector.tensor_copy(picked[:], raw[:].indirect(offsets[:]))
            pairs = picked[:].bitcast(F32)
            turned = turn.tile([P, 2, P], F32, name="turned")
            for u in range(2):
                nc.tensor.transpose(turned[:, u, :], pairs[:, u : 2 * P : 2], ident[:])
            nc.scalar.copy(
                grouped.bitcast(F32).rearrange("p (r u) -> p r u", u=2),
                turned[:].rearrange("p u r -> p r u"),
            )

        g_grouped = keep.tile([P, 4 * N], BF16, name="g_grouped", align_bytes=64)
        x_grouped = [
            keep.tile([P, 4 * P], BF16, name="x_grouped%d" % i, align_bytes=64) for i in range(TILES)
        ]
        g_scales = keep.tile([P, N], U8, name="g_scales", align_bytes=64)

        def multiply(i, codes_tag):
            x_codes = keep.tile([P, P], U32, name="x_codes%d" % i, tag=codes_tag, align_bytes=64)
            x_scales = keep.tile([P, P], U8, name="x_scales%d" % i, align_bytes=64)
            nc.vector.quantize_mx(
                out=x_codes[:].bitcast(E4M3), scales=x_scales[:], in_=x_grouped[i][:]
            )
            w0 = sums.tile([P, N], F32, name="w0_%d" % i)
            nc.tensor.matmul_mx(
                out=w0[:],
                lhsT=x_codes[:].bitcast(E4M3),
                lhsT_scale=x_scales[:],
                rhs=g_codes[:].bitcast(E5M2),
                rhs_scale=g_scales[:],
                start=True,
                stop=True,
            )
            squares = ring.tile([P, N], F32, name="squares")
            total = keep.tile([P, 1], F32, name="total%d" % i)
            nc.scalar.activation(squares[:], w0[:], ACT.Square, scale=0.04, accum_out=total[:])
            gain = keep.tile([P, 1], F32, name="gain%d" % i)
            nc.scalar.activation(
                gain[:], total[:], ACT.Abs_reciprocal_sqrt, bias=floor[:], scale=625.0 / N
            )
            result = keep.tile([P, N], F32, name="result%d" % i)
            half = keep.tile([P, N], F32, name="half%d" % i)
            if i < 2:
                nc.scalar.activation(half[:], w0[:], ACT.Copy, scale=gain[:])
                nc.vector.scalar_tensor_tensor(
                    result[:], old_raw[i][:], -0.1, half[:], ALU.mult, ALU.add
                )
                nc.sync.dma_start(out[rows(i), :], result[:])
            else:
                if i == 2:
                    nc.scalar.activation(half[:], old_raw[i][:], ACT.Copy, scale=0.1)
                else:
                    nc.vector.tensor_scalar_mul(half[:], old_raw[i][:], 0.1)
                pieces = 2 if i == TILES - 1 else 1
                for h in range(pieces):
                    cols = slice(h * N // pieces, (h + 1) * N // pieces)
                    nc.vector.scalar_tensor_tensor(
                        result[:, cols], w0[:, cols], gain[:], half[:, cols], ALU.mult, ALU.subtract
                    )
                    nc.sync.dma_start(out[rows(i), cols], result[:, cols])

        for i in range(TILES):
            gather_and_turn(g_raw[i], g_grouped[:, 4 * P * i : 4 * P * (i + 1)])
        gather_and_turn(x_raw[0], x_grouped[0][:])
        g_codes = keep.tile([P, N], U32, name="g_codes", tag="x0", align_bytes=64)
        nc.vector.quantize_mx(out=g_codes[:].bitcast(E5M2), scales=g_scales[:], in_=g_grouped[:])
        gather_and_turn(x_raw[1], x_grouped[1][:])
        multiply(0, "x1")
        multiply(1, "c1")
        gather_and_turn(x_raw[2], x_grouped[2][:])
        gather_and_turn(x_raw[3], x_grouped[3][:])
        multiply(2, "x3")
        multiply(3, "c3")
